import numpy as np
import ml_dtypes


def mxq(x, axis, fmt="e4m3"):
    dtype, down = {"e4m3": (ml_dtypes.float8_e4m3fn, 7), "e5m2": (ml_dtypes.float8_e5m2, 14)}[fmt]
    v = np.moveaxis(np.asarray(x, np.float32).astype(ml_dtypes.bfloat16).astype(np.float64), axis, -1)
    blocks = v.reshape(v.shape[:-1] + (-1, 32))
    amax = np.abs(blocks).max(-1, keepdims=True)
    byte = np.maximum(np.where(amax > 0, np.frexp(amax)[1] - 1 + 127, 0) - down, 1)
    scale = np.exp2(byte - 127.0)
    codes = (blocks / scale).astype(np.float32).astype(dtype).astype(np.float64)
    return np.moveaxis((codes * scale).reshape(v.shape), -1, axis)


WIDE = False


def mx_kscale(k):
    if not WIDE:
        return np.ones(k)
    levels = np.array([10, -10, 5, -5, 0])
    if k % 512:
        return np.exp2(np.random.permutation(np.resize(levels, k // 32))).repeat(32)
    a = np.empty((k // 512, 16))
    for p in range(k // 512):
        a[p, :8] = np.random.permutation(np.resize(levels, 8))
        for g in range(8):
            far = levels[np.abs(levels - a[p, g]) >= 10]
            a[p, g + 8] = far[np.random.randint(len(far))]
    return np.exp2(a.ravel()).repeat(32)


BF16 = ml_dtypes.bfloat16


def bf(x):
    return np.asarray(x, np.float32).astype(BF16)


def f64(x):
    return np.asarray(x).astype(np.float64)


E2M1 = np.array([0.0, 0.5, 1.0, 1.5, 2.0, 3.0, 4.0, 6.0, -0.0, -0.5, -1.0, -1.5, -2.0, -3.0, -4.0, -6.0])


def pack_weight(w, fmt):
    k, n = w.shape
    w = f64(bf(w)).reshape(k // 32, 32, n)
    amax = np.abs(w).max(1)
    if fmt == "e4m3":
        byte = np.frexp(amax)[1] - 1 + 127 - 7
    else:
        mant, ex = np.frexp(amax / 6.0)
        byte = np.where(mant > 0.5, ex, ex - 1) + 127
    byte = np.clip(np.where(amax > 0, byte, 1), 1, 254)
    scaled = (w * np.exp2(127.0 - byte)[:, None, :]).reshape(k, n).astype(np.float32)
    by_word = np.ascontiguousarray(scaled.reshape(k // 512, 128, 4, n).transpose(0, 1, 3, 2))
    if fmt == "e4m3":
        words = by_word.astype(ml_dtypes.float8_e4m3fn).view(np.uint8)
    else:
        c = by_word.astype(ml_dtypes.float4_e2m1fn).view(np.uint8) & 0xF
        words = c[..., 0::2] | (c[..., 1::2] << 4)
    return np.ascontiguousarray(words), np.ascontiguousarray(byte.astype(np.uint8).reshape(k // 512, 16, n))


def unpack_weight(words, scales, fmt):
    g, p, n, _ = words.shape
    if fmt == "e4m3":
        vals = np.ascontiguousarray(words).view(ml_dtypes.float8_e4m3fn).astype(np.float64)
    else:
        nib = np.empty((g, p, n, 4), np.uint8)
        nib[..., 0::2] = words & 0xF
        nib[..., 1::2] = words >> 4
        vals = E2M1[nib]
    vals = vals * np.repeat(np.exp2(scales.astype(np.float64) - 127.0), 8, axis=1)[..., None]
    return vals.transpose(0, 1, 3, 2).reshape(g * 512, n)
def pack4(w):
    words, scales = pack_weight(w, "e2m1")
    return words.reshape(words.shape[0], 128, -1), scales


def unpack4(words, scales):
    return unpack_weight(words.reshape(words.shape[0], 128, -1, 2), scales, "e2m1")


M, K, N, D = 2048, 1536, 1024, 512


def setup_inputs():
    s = mx_kscale(K)
    t = mx_kscale(N)
    p = np.random.standard_normal((K, M)) * np.exp(0.3 * np.random.standard_normal(M))
    r = np.random.standard_normal((K, N)) * np.exp(0.3 * np.random.standard_normal(N))
    c = np.random.standard_normal((N, D)) / np.sqrt(N)
    p_words, p_scales = pack4(p * s[:, None])
    s_words, s_scales = pack4(r / np.sqrt(K) / s[:, None])
    c_words, c_scales = pack_weight(c / t[:, None], "e4m3")
    return {"p_words": p_words, "p_scales": p_scales,
            "s_words": s_words, "s_scales": s_scales,
            "c_words": c_words, "c_scales": c_scales,
            "inv_p": bf(1.0 / np.mean(p ** 2, axis=0)),
            "inv_s": bf(t / np.mean(r ** 2, axis=0)),
            "base": bf(0.3 * np.random.standard_normal(D))}


def reference(p_words, p_scales, s_words, s_scales, c_words, c_scales, inv_p, inv_s, base):
    P = unpack4(p_words, p_scales)
    S = unpack4(s_words, s_scales)
    C = unpack_weight(c_words, c_scales, "e4m3")
    G = P.T @ S
    H = np.square(G) * f64(inv_s)[None, :]
    Y = mxq(H, 1, "e4m3") @ C
    return Y * f64(inv_p)[:, None] + f64(base)[None, :]

@@ -1,0 +1,236 @@
+from contextlib import ExitStack
+
+import concourse.mybir as mybir
+
+M, K, N, D = 2048, 1536, 1024, 512
+FLOPS = 2 * M * K * N + 2 * M * N * D
+
+F32 = mybir.dt.float32
+BF16 = mybir.dt.bfloat16
+I32 = mybir.dt.int32
+U32 = mybir.dt.uint32
+U8 = mybir.dt.uint8
+FP4X4 = mybir.dt.float4_e2m1fn_x4
+FP8X4 = mybir.dt.float8_e4m3fn_x4
+ACT = mybir.ActivationFunctionType
+ALU = mybir.AluOpType
+
+P = 128
+G = K // 512
+WIDTHS = (512, 512, 512, 256, 256)
+STARTS = tuple(sum(WIDTHS[:k]) for k in range(len(WIDTHS)))
+HALVES = N // 512
+
+
+def tile_soap_kernel_regression_s4_kernel(
+    tc, p_words, p_scales, s_words, s_scales, c_words, c_scales, inv_p, inv_s, base, out
+):
+    nc = tc.nc
+    with ExitStack() as ctx:
+        keep = ctx.enter_context(tc.tile_pool(name="keep", bufs=1))
+        work = ctx.enter_context(tc.tile_pool(name="work", bufs=2))
+        ps1 = ctx.enter_context(tc.psum_pool(name="ps1", bufs=4))
+        ps2 = ctx.enter_context(tc.psum_pool(name="ps2", bufs=4))
+        ctx.enter_context(tc.manual_schedule())
+
+        s_raw = [keep.tile([P, G, 1024], U8, name="s_raw%d" % h, align_bytes=256) for h in range(HALVES)]
+        s_cod = [keep.tile([P, G, 1024], U8, name="s_cod%d" % h, align_bytes=256) for h in range(HALVES)]
+        s_scl = [keep.tile([P, G, 512], U8, name="s_scl%d" % h, align_bytes=256) for h in range(HALVES)]
+        s_scr = keep.tile([P, G, N], U8, name="s_scr", align_bytes=256)
+        p_cod = [keep.tile([P, G, 1024], U8, name="p_cod%d" % c, align_bytes=256) for c in range(4)]
+        p_sc0 = keep.tile([P, G, 512], U8, name="p_sc0", align_bytes=256)
+        p_scr = keep.tile([P, G, M - 512], U8, name="p_scr", align_bytes=256)
+        c_cod = keep.tile([P, HALVES, 4 * D], U8, name="c_cod", align_bytes=256)
+        c_scl = keep.tile([P, HALVES, D], U8, name="c_scl", align_bytes=256)
+        ivs = keep.tile([P, HALVES, 4], BF16, name="ivs")
+        rts = keep.tile([P, HALVES, 4], F32, name="rts")
+        ivp = keep.tile([P, 16], BF16, name="ivp")
+        ivq = keep.tile([P, 16], BF16, name="ivq")
+        ivpf = keep.tile([P, 16], F32, name="ivpf")
+        bas = keep.tile([P, D], BF16, name="bas", align_bytes=64)
+        warm = keep.tile([P, 1], F32, name="warm")
+
+        def load_scales(queues, plane, rows, n0, n1):
+            for q in range(4):
+                queues[q].dma_start(
+                    out=plane[32 * q : 32 * q + 4, :, :].bitcast(I32),
+                    in_=rows[:, 4 * q : 4 * q + 4, n0:n1].bitcast(I32).rearrange("g r n -> r g n"),
+                )
+
+        def load_words(tile, rows, b0, b1):
+            nc.sync.dma_start(
+                out=tile[:].bitcast(I32), in_=rows[:, :, b0:b1].bitcast(I32).rearrange("g p n -> p g n")
+            )
+
+        sy, ac, gp = nc.sync, nc.scalar, nc.gpsimd
+        nc.vector.memset(s_scr[:].bitcast(I32), 0)
+        nc.gpsimd.memset(p_sc0[:].bitcast(I32), 0)
+        nc.vector.memset(warm[:], 1.0)
+        load_words(s_raw[0], s_words, 0, 1024)
+        load_words(p_cod[0], p_words, 0, 1024)
+        load_scales((sy, sy, sy, sy), s_scr, s_scales, 0, N)
+        load_scales((ac, ac, gp, gp), p_sc0, p_scales, 0, 512)
+        nc.gpsimd.dma_start(out=ivs[:], in_=inv_s.rearrange("(h p t) -> p h t", h=HALVES, t=4))
+        nc.gpsimd.memset(p_scr[:].bitcast(I32), 0)
+        nc.gpsimd.memset(c_scl[:].bitcast(I32), 0)
+        nc.scalar.activation(out=warm[:], in_=warm[:], func=ACT.Sqrt)
+        load_words(s_raw[1], s_words, 1024, 2048)
+        load_words(p_cod[1], p_words, 1024, 2048)
+        load_scales((sy, sy, sy, sy), p_scr, p_scales, 512, M)
+        load_scales((sy, sy, sy, sy), c_scl, c_scales, 0, D)
+        nc.sync.dma_start(
+            out=c_cod[:].bitcast(I32),
+            in_=c_words.rearrange("g p n t -> g p (n t)").bitcast(I32).rearrange("g p n -> p g n"),
+        )
+        nc.sync.dma_start(
+            out=ivp[:, 0:12].rearrange("p (c i) -> p c i", i=4),
+            in_=inv_p[0:1536].rearrange("(c p i) -> p c i", c=3, i=4),
+        )
+        nc.sync.dma_start(
+            out=ivq[:, 0:4].rearrange("p (c i) -> p c i", i=2),
+            in_=inv_p[1536:2048].rearrange("(c p i) -> p c i", c=2, i=2),
+        )
+        nc.sync.dma_start(out=bas[:], in_=base.partition_broadcast(P))
+        load_words(p_cod[2], p_words, 2048, 3072)
+        load_words(p_cod[3], p_words, 3072, 4096)
+        nc.scalar.activation(out=rts[:], in_=ivs[:], func=ACT.Sqrt)
+
+        def permute(h, t):
+            nc.vector.tensor_copy(
+                out=s_scl[h][:, :, 128 * t : 128 * t + 128],
+                in_=s_scr[:, :, 512 * h : 512 * h + 512].rearrange("k g (m t) -> k g t m", t=4)[:, :, t, :],
+            )
+            nc.vector.tensor_copy(
+                out=s_cod[h][:, :, 256 * t : 256 * t + 256].rearrange("k g (m b) -> k g m b", b=2),
+                in_=s_raw[h][:].rearrange("k g (m t b) -> k g t m b", t=4, b=2)[:, :, t, :, :],
+            )
+
+        flat = {}
+        mixed = {}
+        codes = {}
+        scales = {}
+
+        def stage1(h, t, k):
+            width, start = WIDTHS[k], STARTS[k]
+            cell, off = divmod(start, 512)
+            acc = ps1.tile([P, 512], F32, name="acc")
+            for g in range(G):
+                psc = p_sc0[:, g, :] if start == 0 else p_scr[:, g, start - 512 : start - 512 + width]
+                nc.tensor.matmul_mx(
+                    out=acc[:, 0:width],
+                    lhsT=s_cod[h][:, g, 256 * t : 256 * t + 256].bitcast(FP4X4),
+                    lhsT_scale=s_scl[h][:, g, 128 * t : 128 * t + 128],
+                    rhs=p_cod[cell][:, g, 2 * off : 2 * (off + width)].bitcast(FP4X4),
+                    rhs_scale=psc,
+                    start=(g == 0),
+                    stop=(g == G - 1),
+                )
+            if t == 0:
+                flat[h, k] = work.tile([P, 4, 512], BF16, name="flat", bufs=3, align_bytes=64)
+            nt = width // 128
+            nc.scalar.activation(
+                out=flat[h, k][:, t, 0:width].rearrange("k (i p) -> k i p", i=nt),
+                in_=acc[:, 0:width].rearrange("k (p i) -> k i p", i=nt),
+                func=ACT.Square,
+                scale=rts[:, h, t : t + 1],
+            )
+
+        def mix_tile(h, k):
+            mixed[h, k] = work.tile([P, 512, 4], BF16, name="mixed", bufs=3, align_bytes=64)
+            codes[h, k] = work.tile([P, 512], U32, name="codes%d" % h, bufs=2, align_bytes=256)
+            scales[h, k] = work.tile([P, 512], U8, name="scales%d" % h, bufs=2, align_bytes=256)
+
+        def mix(engine_copy, h, k, i0, i1):
+            cols = slice(128 * i0, 128 * i1)
+            engine_copy(
+                out=mixed[h, k][:, cols, :],
+                in_=flat[h, k][:, :, cols].rearrange("k t m -> k m t"),
+            )
+
+        def quantize(h, k, i0, i1):
+            cols = slice(128 * i0, 128 * i1)
+            nc.vector.quantize_mx(
+                out=codes[h, k][:, cols].bitcast(FP8X4),
+                scales=scales[h, k][:, cols],
+                in_=mixed[h, k][:, cols, :].rearrange("k m t -> k (m t)"),
+            )
+
+        ys = {}
+
+        def stage2_pass(k, i, h):
+            if h == 0:
+                ys[k, i] = ps2.tile([P, D], F32, name="y")
+            cols = slice(128 * i, 128 * i + 128)
+            nc.tensor.matmul_mx(
+                out=ys[k, i][:],
+                lhsT=codes[h, k][:, cols].bitcast(FP8X4),
+                lhsT_scale=scales[h, k][:, cols],
+                rhs=c_cod[:, h, :].bitcast(FP8X4),
+                rhs_scale=c_scl[:, h, :],
+                start=(h == 0),
+                stop=(h == HALVES - 1),
+            )
+
+        def stage2_out(k, i):
+            nt = WIDTHS[k] // 128
+            col = STARTS[k] // 128 + i
+            res = work.tile([P, D], F32, name="res", bufs=6, align_bytes=64)
+            nc.vector.scalar_tensor_tensor(
+                out=res[:], in0=ys[k, i][:], scalar=ivpf[:, col : col + 1], in1=bas[:], op0=ALU.mult, op1=ALU.add
+            )
+            rows = out[STARTS[k] : STARTS[k] + WIDTHS[k], :].rearrange("(p i) d -> i p d", i=nt)
+            nc.sync.dma_start(out=rows[i], in_=res[:])
+
+        def stage2(k, i):
+            stage2_pass(k, i, 0)
+            stage2_pass(k, i, 1)
+            stage2_out(k, i)
+
+        finish = {
+            (1, 3): (0, 0), (1, 4): (0, 1), (1, 6): (0, 2), (1, 7): (0, 3),
+            (2, 3): (1, 0), (2, 4): (1, 1), (2, 6): (1, 2), (2, 7): (1, 3),
+            (3, 5): (2, 0), (3, 7): (2, 1), (4, 1): (2, 2), (4, 3): (2, 3),
+            (4, 6): (3, 0), (4, 7): (3, 1),
+        }
+        last = len(WIDTHS) - 1
+        for t in range(4):
+            permute(0, t)
+        for k in range(len(WIDTHS)):
+            nt = WIDTHS[k] // 128
+            for s in range(8):
+                h, t = divmod(s, 4)
+                if k == 0 and s < 4:
+                    permute(1, s)
+                if s == 5:
+                    mix_tile(0, k)
+                    if nt == 4:
+                        mix(nc.scalar.copy, 0, k, 3, 4)
+                if s == 1 and k > 0:
+                    mix_tile(1, k - 1)
+                    if WIDTHS[k - 1] == 512:
+                        mix(nc.scalar.copy, 1, k - 1, 3, 4)
+                stage1(h, t, k)
+                if s == 5:
+                    mix(nc.vector.tensor_copy, 0, k, 0, min(nt, 3))
+                if s == 6:
+                    quantize(0, k, 0, nt)
+                if k == 0 and s == 7:
+                    nc.vector.tensor_copy(out=ivpf[:, 0:12], in_=ivp[:, 0:12])
+                    nc.vector.tensor_copy(out=ivpf[:, 12:16], in_=ivq[:, 0:4])
+                if k > 0:
+                    if s == 1:
+                        mix(nc.vector.tensor_copy, 1, k - 1, 0, min(WIDTHS[k - 1] // 128, 3))
+                    if s == 2:
+                        quantize(1, k - 1, 0, WIDTHS[k - 1] // 128)
+                if (k, s) in finish:
+                    stage2(*finish[k, s])
+        mix_tile(1, last)
+        mix(nc.vector.tensor_copy, 1, last, 0, 1)
+        mix(nc.scalar.copy, 1, last, 1, 2)
+        for i in range(2):
+            stage2_pass(last, i, 0)
+        for i in range(2):
+            quantize(1, last, i, i + 1)
+            stage2_pass(last, i, 1)
+        for i in range(2):
+            stage2_out(last, i)

@@ -17,9 +17,8 @@ ALU = mybir.AluOpType
 
 P = 128
 G = K // 512
-WIDTHS = (512, 512, 512, 256, 256)
-STARTS = tuple(sum(WIDTHS[:k]) for k in range(len(WIDTHS)))
 HALVES = N // 512
+CHUNKS = M // 512
 
 
 def tile_soap_kernel_regression_s4_kernel(
@@ -35,11 +34,12 @@ def tile_soap_kernel_regression_s4_kernel(
 
         s_raw = [keep.tile([P, G, 1024], U8, name="s_raw%d" % h, align_bytes=256) for h in range(HALVES)]
         s_cod = [keep.tile([P, G, 1024], U8, name="s_cod%d" % h, align_bytes=256) for h in range(HALVES)]
+        s_scr = [keep.tile([P, G, 512], U8, name="s_scr%d" % h, align_bytes=256) for h in range(HALVES)]
         s_scl = [keep.tile([P, G, 512], U8, name="s_scl%d" % h, align_bytes=256) for h in range(HALVES)]
-        s_scr = keep.tile([P, G, N], U8, name="s_scr", align_bytes=256)
-        p_cod = [keep.tile([P, G, 1024], U8, name="p_cod%d" % c, align_bytes=256) for c in range(4)]
+        p_cod = [keep.tile([P, G, 1024], U8, name="p_cod%d" % c, align_bytes=256) for c in range(CHUNKS)]
         p_sc0 = keep.tile([P, G, 512], U8, name="p_sc0", align_bytes=256)
-        p_scr = keep.tile([P, G, M - 512], U8, name="p_scr", align_bytes=256)
+        p_sc1 = keep.tile([P, G, 512], U8, name="p_sc1", align_bytes=256)
+        p_sc2 = keep.tile([P, G, 1024], U8, name="p_sc2", align_bytes=256)
         c_cod = keep.tile([P, HALVES, 4 * D], U8, name="c_cod", align_bytes=256)
         c_scl = keep.tile([P, HALVES, D], U8, name="c_scl", align_bytes=256)
         ivs = keep.tile([P, HALVES, 4], BF16, name="ivs")
@@ -63,20 +63,24 @@ def tile_soap_kernel_regression_s4_kernel(
             )
 
         sy, ac, gp = nc.sync, nc.scalar, nc.gpsimd
-        nc.vector.memset(s_scr[:].bitcast(I32), 0)
-        nc.gpsimd.memset(p_sc0[:].bitcast(I32), 0)
-        nc.vector.memset(warm[:], 1.0)
         load_words(s_raw[0], s_words, 0, 1024)
+        nc.vector.memset(s_scr[0][:].bitcast(I32), 0)
+        nc.gpsimd.memset(p_sc0[:].bitcast(I32), 0)
+        load_scales((sy, sy, sy, sy), s_scr[0], s_scales, 0, 512)
         load_words(p_cod[0], p_words, 0, 1024)
-        load_scales((sy, sy, sy, sy), s_scr, s_scales, 0, N)
         load_scales((ac, ac, gp, gp), p_sc0, p_scales, 0, 512)
         nc.gpsimd.dma_start(out=ivs[:], in_=inv_s.rearrange("(h p t) -> p h t", h=HALVES, t=4))
-        nc.gpsimd.memset(p_scr[:].bitcast(I32), 0)
-        nc.gpsimd.memset(c_scl[:].bitcast(I32), 0)
+        nc.vector.memset(warm[:], 1.0)
+        nc.vector.memset(p_sc1[:].bitcast(I32), 0)
+        nc.vector.memset(s_scr[1][:].bitcast(I32), 0)
+        nc.vector.memset(p_sc2[:].bitcast(I32), 0)
+        nc.vector.memset(c_scl[:].bitcast(I32), 0)
         nc.scalar.activation(out=warm[:], in_=warm[:], func=ACT.Sqrt)
-        load_words(s_raw[1], s_words, 1024, 2048)
         load_words(p_cod[1], p_words, 1024, 2048)
-        load_scales((sy, sy, sy, sy), p_scr, p_scales, 512, M)
+        load_scales((sy, sy, sy, sy), p_sc1, p_scales, 512, 1024)
+        load_words(s_raw[1], s_words, 1024, 2048)
+        load_scales((sy, sy, sy, sy), s_scr[1], s_scales, 512, 1024)
+        load_scales((sy, sy, sy, sy), p_sc2, p_scales, 1024, M)
         load_scales((sy, sy, sy, sy), c_scl, c_scales, 0, D)
         nc.sync.dma_start(
             out=c_cod[:].bitcast(I32),
@@ -98,139 +102,170 @@ def tile_soap_kernel_regression_s4_kernel(
         def permute(h, t):
             nc.vector.tensor_copy(
                 out=s_scl[h][:, :, 128 * t : 128 * t + 128],
-                in_=s_scr[:, :, 512 * h : 512 * h + 512].rearrange("k g (m t) -> k g t m", t=4)[:, :, t, :],
+                in_=s_scr[h][:].rearrange("k g (m t) -> k g t m", t=4)[:, :, t, :],
             )
             nc.vector.tensor_copy(
                 out=s_cod[h][:, :, 256 * t : 256 * t + 256].rearrange("k g (m b) -> k g m b", b=2),
                 in_=s_raw[h][:].rearrange("k g (m t b) -> k g t m b", t=4, b=2)[:, :, t, :, :],
             )
 
-        flat = {}
-        mixed = {}
-        codes = {}
-        scales = {}
+        flat, mixed, codes, scales, ys = {}, {}, {}, {}, {}
 
-        def stage1(h, t, k):
-            width, start = WIDTHS[k], STARTS[k]
-            cell, off = divmod(start, 512)
+        def warm_up():
+            dummy = ps2.tile([P, D], F32, name="y")
+            nc.tensor.matmul_mx(
+                out=dummy[:],
+                lhsT=s_raw[0][:, 0, 0:256].bitcast(FP4X4),
+                lhsT_scale=s_scr[0][:, 0, 0:128],
+                rhs=s_raw[0][:, 0, :].bitcast(FP4X4),
+                rhs_scale=s_scr[0][:, 0, :],
+                start=True,
+                stop=True,
+            )
+
+        def p_scale(c, g, x0, x1):
+            if c < 2:
+                return (p_sc0, p_sc1)[c][:, g, x0:x1]
+            return p_sc2[:, g, 512 * (c - 2) + x0 : 512 * (c - 2) + x1]
+
+        def stage1(c, h, t, x0, x1):
             acc = ps1.tile([P, 512], F32, name="acc")
             for g in range(G):
-                psc = p_sc0[:, g, :] if start == 0 else p_scr[:, g, start - 512 : start - 512 + width]
                 nc.tensor.matmul_mx(
-                    out=acc[:, 0:width],
+                    out=acc[:, 0 : x1 - x0],
                     lhsT=s_cod[h][:, g, 256 * t : 256 * t + 256].bitcast(FP4X4),
                     lhsT_scale=s_scl[h][:, g, 128 * t : 128 * t + 128],
-                    rhs=p_cod[cell][:, g, 2 * off : 2 * (off + width)].bitcast(FP4X4),
-                    rhs_scale=psc,
+                    rhs=p_cod[c][:, g, 2 * x0 : 2 * x1].bitcast(FP4X4),
+                    rhs_scale=p_scale(c, g, x0, x1),
                     start=(g == 0),
                     stop=(g == G - 1),
                 )
-            if t == 0:
-                flat[h, k] = work.tile([P, 4, 512], BF16, name="flat", bufs=3, align_bytes=64)
-            nt = width // 128
+            if t == 0 and x0 == 0:
+                flat[c, h] = work.tile([P, 4, 512], BF16, name="flat", bufs=6, align_bytes=64)
+                mixed[c, h] = work.tile([P, 512, 4], BF16, name="mixed", bufs=6, align_bytes=64)
+                codes[c, h] = work.tile([P, 512], U32, name="codes%d" % h, bufs=4, align_bytes=256)
+                scales[c, h] = work.tile([P, 512], U8, name="scales%d" % h, bufs=4, align_bytes=256)
+            nt = 4 if c < 3 else 2
             nc.scalar.activation(
-                out=flat[h, k][:, t, 0:width].rearrange("k (i p) -> k i p", i=nt),
-                in_=acc[:, 0:width].rearrange("k (p i) -> k i p", i=nt),
+                out=flat[c, h][:, t, x0:x1].rearrange("k (x i p) -> k x i p", i=nt, p=P),
+                in_=acc[:, 0 : x1 - x0].rearrange("k (x p i) -> k x i p", i=nt, p=P),
                 func=ACT.Square,
                 scale=rts[:, h, t : t + 1],
             )
 
-        def mix_tile(h, k):
-            mixed[h, k] = work.tile([P, 512, 4], BF16, name="mixed", bufs=3, align_bytes=64)
-            codes[h, k] = work.tile([P, 512], U32, name="codes%d" % h, bufs=2, align_bytes=256)
-            scales[h, k] = work.tile([P, 512], U8, name="scales%d" % h, bufs=2, align_bytes=256)
-
-        def mix(engine_copy, h, k, i0, i1):
-            cols = slice(128 * i0, 128 * i1)
+        def mix(engine_copy, c, h, j0, j1):
+            cols = slice(128 * j0, 128 * j1)
             engine_copy(
-                out=mixed[h, k][:, cols, :],
-                in_=flat[h, k][:, :, cols].rearrange("k t m -> k m t"),
+                out=mixed[c, h][:, cols, :],
+                in_=flat[c, h][:, :, cols].rearrange("k t m -> k m t"),
             )
 
-        def quantize(h, k, i0, i1):
-            cols = slice(128 * i0, 128 * i1)
+        def ma(c, h, j):
+            mix(nc.scalar.copy, c, h, j, j + 1)
+
+        def mv(c, h, j0, j1):
+            mix(nc.vector.tensor_copy, c, h, j0, j1)
+
+        def q(c, h, j0, j1):
+            cols = slice(128 * j0, 128 * j1)
             nc.vector.quantize_mx(
-                out=codes[h, k][:, cols].bitcast(FP8X4),
-                scales=scales[h, k][:, cols],
-                in_=mixed[h, k][:, cols, :].rearrange("k m t -> k (m t)"),
+                out=codes[c, h][:, cols].bitcast(FP8X4),
+                scales=scales[c, h][:, cols],
+                in_=mixed[c, h][:, cols, :].rearrange("k m t -> k (m t)"),
             )
 
-        ys = {}
-
-        def stage2_pass(k, i, h):
+        def stage2_pass(c, j, h):
             if h == 0:
-                ys[k, i] = ps2.tile([P, D], F32, name="y")
-            cols = slice(128 * i, 128 * i + 128)
+                ys[c, j] = ps2.tile([P, D], F32, name="y")
+            cols = slice(128 * j, 128 * j + 128)
             nc.tensor.matmul_mx(
-                out=ys[k, i][:],
-                lhsT=codes[h, k][:, cols].bitcast(FP8X4),
-                lhsT_scale=scales[h, k][:, cols],
+                out=ys[c, j][:],
+                lhsT=codes[c, h][:, cols].bitcast(FP8X4),
+                lhsT_scale=scales[c, h][:, cols],
                 rhs=c_cod[:, h, :].bitcast(FP8X4),
                 rhs_scale=c_scl[:, h, :],
                 start=(h == 0),
                 stop=(h == HALVES - 1),
             )
 
-        def stage2_out(k, i):
-            nt = WIDTHS[k] // 128
-            col = STARTS[k] // 128 + i
+        def p2a(c, j):
+            stage2_pass(c, j, 0)
+
+        def p2b(c, j):
+            stage2_pass(c, j, 1)
+
+        def out_cols(c, j, d0, d1):
             res = work.tile([P, D], F32, name="res", bufs=6, align_bytes=64)
             nc.vector.scalar_tensor_tensor(
-                out=res[:], in0=ys[k, i][:], scalar=ivpf[:, col : col + 1], in1=bas[:], op0=ALU.mult, op1=ALU.add
+                out=res[:, d0:d1], in0=ys[c, j][:, d0:d1], scalar=ivpf[:, 4 * c + j : 4 * c + j + 1],
+                in1=bas[:, d0:d1], op0=ALU.mult, op1=ALU.add,
             )
-            rows = out[STARTS[k] : STARTS[k] + WIDTHS[k], :].rearrange("(p i) d -> i p d", i=nt)
-            nc.sync.dma_start(out=rows[i], in_=res[:])
+            if c < 3:
+                rows = out[512 * c : 512 * c + 512, :].rearrange("(p i) d -> i p d", i=4)[j]
+            else:
+                x = 512 * c + 256 * (j // 2)
+                rows = out[x : x + 256, :].rearrange("(p i) d -> i p d", i=2)[j % 2]
+            nc.sync.dma_start(out=rows[:, d0:d1], in_=res[:, d0:d1])
 
-        def stage2(k, i):
-            stage2_pass(k, i, 0)
-            stage2_pass(k, i, 1)
-            stage2_out(k, i)
+        def out_tile(c, j):
+            out_cols(c, j, 0, D)
 
-        finish = {
-            (1, 3): (0, 0), (1, 4): (0, 1), (1, 6): (0, 2), (1, 7): (0, 3),
-            (2, 3): (1, 0), (2, 4): (1, 1), (2, 6): (1, 2), (2, 7): (1, 3),
-            (3, 5): (2, 0), (3, 7): (2, 1), (4, 1): (2, 2), (4, 3): (2, 3),
-            (4, 6): (3, 0), (4, 7): (3, 1),
+        def s2(c, j):
+            p2a(c, j)
+            p2b(c, j)
+            out_tile(c, j)
+
+        def widen():
+            nc.vector.tensor_copy(out=ivpf[:, 0:12], in_=ivp[:, 0:12])
+            nc.vector.tensor_copy(out=ivpf[:, 12:16], in_=ivq[:, 0:4])
+
+        first = [(0, 0), (0, 1), (1, 0), (1, 1)] + [(c, s) for s in range(2, 8) for c in (0, 1)]
+        groups = [(c, s // 4, s % 4, 0, 512) for c, s in first]
+        groups += [(2, s // 4, s % 4, 0, 512) for s in range(8)]
+        groups += [(3, 0, t, 0, 512) for t in range(4)]
+        groups += [(3, 1, t, x, x + 256) for x in (0, 256) for t in range(4)]
+        after = {
+            7: [(ma, 0, 0, 2)],
+            8: [(ma, 0, 0, 3), (mv, 0, 0, 0, 2)],
+            9: [(ma, 1, 0, 2)],
+            10: [(ma, 1, 0, 3), (mv, 1, 0, 0, 2)],
+            11: [(q, 0, 0, 0, 4)],
+            12: [(q, 1, 0, 0, 4)],
+            15: [(ma, 0, 1, 3), (mv, 0, 1, 0, 3)],
+            16: [(ma, 1, 1, 3), (widen,)],
+            17: [(q, 0, 1, 0, 4), (mv, 1, 1, 0, 3)],
+            18: [(q, 1, 1, 0, 4)],
+            19: [(s2, 0, 0), (s2, 0, 1), (ma, 2, 0, 2)],
+            20: [(mv, 2, 0, 0, 2), (ma, 2, 0, 3), (s2, 0, 2)],
+            21: [(s2, 0, 3)],
+            22: [(q, 2, 0, 0, 4), (s2, 1, 0)],
+            23: [(s2, 1, 1), (ma, 2, 1, 2)],
+            24: [(mv, 2, 1, 0, 2), (ma, 2, 1, 3), (s2, 1, 2)],
+            25: [(q, 2, 1, 0, 4), (s2, 1, 3)],
+            26: [(s2, 2, 0)],
+            27: [(ma, 3, 0, 2)],
+            28: [(mv, 3, 0, 0, 2), (ma, 3, 0, 3)],
+            29: [(s2, 2, 1)],
+            30: [(q, 3, 0, 0, 4)],
+            31: [(s2, 2, 2)],
+            32: [(mv, 3, 1, 0, 2)],
+            33: [(s2, 2, 3)],
+            34: [(q, 3, 1, 0, 2)],
+            35: [
+                (ma, 3, 1, 3), (mv, 3, 1, 2, 3),
+                (p2a, 3, 0), (p2b, 3, 0), (p2a, 3, 1), (p2b, 3, 1), (p2a, 3, 2), (p2a, 3, 3),
+                (out_tile, 3, 0), (q, 3, 1, 2, 3), (p2b, 3, 2), (q, 3, 1, 3, 4), (p2b, 3, 3),
+                (out_tile, 3, 1), (out_tile, 3, 2), (out_cols, 3, 3, 0, 256), (out_cols, 3, 3, 256, 512),
+            ],
         }
-        last = len(WIDTHS) - 1
-        for t in range(4):
-            permute(0, t)
-        for k in range(len(WIDTHS)):
-            nt = WIDTHS[k] // 128
-            for s in range(8):
-                h, t = divmod(s, 4)
-                if k == 0 and s < 4:
-                    permute(1, s)
-                if s == 5:
-                    mix_tile(0, k)
-                    if nt == 4:
-                        mix(nc.scalar.copy, 0, k, 3, 4)
-                if s == 1 and k > 0:
-                    mix_tile(1, k - 1)
-                    if WIDTHS[k - 1] == 512:
-                        mix(nc.scalar.copy, 1, k - 1, 3, 4)
-                stage1(h, t, k)
-                if s == 5:
-                    mix(nc.vector.tensor_copy, 0, k, 0, min(nt, 3))
-                if s == 6:
-                    quantize(0, k, 0, nt)
-                if k == 0 and s == 7:
-                    nc.vector.tensor_copy(out=ivpf[:, 0:12], in_=ivp[:, 0:12])
-                    nc.vector.tensor_copy(out=ivpf[:, 12:16], in_=ivq[:, 0:4])
-                if k > 0:
-                    if s == 1:
-                        mix(nc.vector.tensor_copy, 1, k - 1, 0, min(WIDTHS[k - 1] // 128, 3))
-                    if s == 2:
-                        quantize(1, k - 1, 0, WIDTHS[k - 1] // 128)
-                if (k, s) in finish:
-                    stage2(*finish[k, s])
-        mix_tile(1, last)
-        mix(nc.vector.tensor_copy, 1, last, 0, 1)
-        mix(nc.scalar.copy, 1, last, 1, 2)
-        for i in range(2):
-            stage2_pass(last, i, 0)
-        for i in range(2):
-            quantize(1, last, i, i + 1)
-            stage2_pass(last, i, 1)
-        for i in range(2):
-            stage2_out(last, i)
+        permute(0, 0)
+        for n in range(3):
+            warm_up()
+        for h in range(HALVES):
+            for t in range(4):
+                if (h, t) != (0, 0):
+                    permute(h, t)
+        for n, group in enumerate(groups):
+            stage1(*group)
+            for step in after.get(n, []):
+                step[0](*step[1:])

from contextlib import ExitStack

import concourse.mybir as mybir

M, K, N, D = 2048, 1536, 1024, 512
FLOPS = 2 * M * K * N + 2 * M * N * D

F32 = mybir.dt.float32
BF16 = mybir.dt.bfloat16
I32 = mybir.dt.int32
U32 = mybir.dt.uint32
U8 = mybir.dt.uint8
FP4X4 = mybir.dt.float4_e2m1fn_x4
FP8X4 = mybir.dt.float8_e4m3fn_x4
ACT = mybir.ActivationFunctionType
ALU = mybir.AluOpType

P = 128
G = K // 512
HALVES = N // 512
CHUNKS = M // 512


def tile_soap_kernel_regression_s4_kernel(
    tc, p_words, p_scales, s_words, s_scales, c_words, c_scales, inv_p, inv_s, base, out
):
    nc = tc.nc
    with ExitStack() as ctx:
        keep = ctx.enter_context(tc.tile_pool(name="keep", bufs=1))
        work = ctx.enter_context(tc.tile_pool(name="work", bufs=2))
        ps1 = ctx.enter_context(tc.psum_pool(name="ps1", bufs=4))
        ps2 = ctx.enter_context(tc.psum_pool(name="ps2", bufs=4))
        ctx.enter_context(tc.manual_schedule())

        s_raw = [keep.tile([P, G, 1024], U8, name="s_raw%d" % h, align_bytes=256) for h in range(HALVES)]
        s_cod = [keep.tile([P, G, 1024], U8, name="s_cod%d" % h, align_bytes=256) for h in range(HALVES)]
        s_scr = [keep.tile([P, G, 512], U8, name="s_scr%d" % h, align_bytes=256) for h in range(HALVES)]
        s_scl = [keep.tile([P, G, 512], U8, name="s_scl%d" % h, align_bytes=256) for h in range(HALVES)]
        p_cod = [keep.tile([P, G, 1024], U8, name="p_cod%d" % c, align_bytes=256) for c in range(CHUNKS)]
        p_sc0 = keep.tile([P, G, 512], U8, name="p_sc0", align_bytes=256)
        p_sc1 = keep.tile([P, G, 512], U8, name="p_sc1", align_bytes=256)
        p_sc2 = keep.tile([P, G, 1024], U8, name="p_sc2", align_bytes=256)
        c_cod = keep.tile([P, HALVES, 4 * D], U8, name="c_cod", align_bytes=256)
        c_scl = keep.tile([P, HALVES, D], U8, name="c_scl", align_bytes=256)
        ivs = keep.tile([P, HALVES, 4], BF16, name="ivs")
        rts = keep.tile([P, HALVES, 4], F32, name="rts")
        ivp = keep.tile([P, 16], BF16, name="ivp")
        ivq = keep.tile([P, 16], BF16, name="ivq")
        ivpf = keep.tile([P, 16], F32, name="ivpf")
        bas = keep.tile([P, D], BF16, name="bas", align_bytes=64)
        warm = keep.tile([P, 1], F32, name="warm")

        def load_scales(queues, plane, rows, n0, n1):
            for q in range(4):
                queues[q].dma_start(
                    out=plane[32 * q : 32 * q + 4, :, :].bitcast(I32),
                    in_=rows[:, 4 * q : 4 * q + 4, n0:n1].bitcast(I32).rearrange("g r n -> r g n"),
                )

        def load_words(tile, rows, b0, b1):
            nc.sync.dma_start(
                out=tile[:].bitcast(I32), in_=rows[:, :, b0:b1].bitcast(I32).rearrange("g p n -> p g n")
            )

        sy, ac, gp = nc.sync, nc.scalar, nc.gpsimd
        load_words(s_raw[0], s_words, 0, 1024)
        nc.vector.memset(s_scr[0][:].bitcast(I32), 0)
        nc.gpsimd.memset(p_sc0[:].bitcast(I32), 0)
        load_scales((sy, sy, sy, sy), s_scr[0], s_scales, 0, 512)
        load_words(p_cod[0], p_words, 0, 1024)
        load_scales((ac, ac, gp, gp), p_sc0, p_scales, 0, 512)
        nc.gpsimd.dma_start(out=ivs[:], in_=inv_s.rearrange("(h p t) -> p h t", h=HALVES, t=4))
        nc.vector.memset(warm[:], 1.0)
        nc.vector.memset(p_sc1[:].bitcast(I32), 0)
        nc.vector.memset(s_scr[1][:].bitcast(I32), 0)
        nc.vector.memset(p_sc2[:].bitcast(I32), 0)
        nc.vector.memset(c_scl[:].bitcast(I32), 0)
        nc.scalar.activation(out=warm[:], in_=warm[:], func=ACT.Sqrt)
        load_words(p_cod[1], p_words, 1024, 2048)
        load_scales((sy, sy, sy, sy), p_sc1, p_scales, 512, 1024)
        load_words(s_raw[1], s_words, 1024, 2048)
        load_scales((sy, sy, sy, sy), s_scr[1], s_scales, 512, 1024)
        load_scales((sy, sy, sy, sy), p_sc2, p_scales, 1024, M)
        load_scales((sy, sy, sy, sy), c_scl, c_scales, 0, D)
        nc.sync.dma_start(
            out=c_cod[:].bitcast(I32),
            in_=c_words.rearrange("g p n t -> g p (n t)").bitcast(I32).rearrange("g p n -> p g n"),
        )
        nc.sync.dma_start(
            out=ivp[:, 0:12].rearrange("p (c i) -> p c i", i=4),
            in_=inv_p[0:1536].rearrange("(c p i) -> p c i", c=3, i=4),
        )
        nc.sync.dma_start(
            out=ivq[:, 0:4].rearrange("p (c i) -> p c i", i=2),
            in_=inv_p[1536:2048].rearrange("(c p i) -> p c i", c=2, i=2),
        )
        nc.sync.dma_start(out=bas[:], in_=base.partition_broadcast(P))
        load_words(p_cod[2], p_words, 2048, 3072)
        load_words(p_cod[3], p_words, 3072, 4096)
        nc.scalar.activation(out=rts[:], in_=ivs[:], func=ACT.Sqrt)

        def permute(h, t):
            nc.vector.tensor_copy(
                out=s_scl[h][:, :, 128 * t : 128 * t + 128],
                in_=s_scr[h][:].rearrange("k g (m t) -> k g t m", t=4)[:, :, t, :],
            )
            nc.vector.tensor_copy(
                out=s_cod[h][:, :, 256 * t : 256 * t + 256].rearrange("k g (m b) -> k g m b", b=2),
                in_=s_raw[h][:].rearrange("k g (m t b) -> k g t m b", t=4, b=2)[:, :, t, :, :],
            )

        flat, mixed, codes, scales, ys = {}, {}, {}, {}, {}

        def warm_up():
            dummy = ps2.tile([P, D], F32, name="y")
            nc.tensor.matmul_mx(
                out=dummy[:],
                lhsT=s_raw[0][:, 0, 0:256].bitcast(FP4X4),
                lhsT_scale=s_scr[0][:, 0, 0:128],
                rhs=s_raw[0][:, 0, :].bitcast(FP4X4),
                rhs_scale=s_scr[0][:, 0, :],
                start=True,
                stop=True,
            )

        def p_scale(c, g, x0, x1):
            if c < 2:
                return (p_sc0, p_sc1)[c][:, g, x0:x1]
            return p_sc2[:, g, 512 * (c - 2) + x0 : 512 * (c - 2) + x1]

        def stage1(c, h, t, x0, x1):
            acc = ps1.tile([P, 512], F32, name="acc")
            for g in range(G):
                nc.tensor.matmul_mx(
                    out=acc[:, 0 : x1 - x0],
                    lhsT=s_cod[h][:, g, 256 * t : 256 * t + 256].bitcast(FP4X4),
                    lhsT_scale=s_scl[h][:, g, 128 * t : 128 * t + 128],
                    rhs=p_cod[c][:, g, 2 * x0 : 2 * x1].bitcast(FP4X4),
                    rhs_scale=p_scale(c, g, x0, x1),
                    start=(g == 0),
                    stop=(g == G - 1),
                )
            if t == 0 and x0 == 0:
                flat[c, h] = work.tile([P, 4, 512], BF16, name="flat", bufs=6, align_bytes=64)
                mixed[c, h] = work.tile([P, 512, 4], BF16, name="mixed", bufs=6, align_bytes=64)
                codes[c, h] = work.tile([P, 512], U32, name="codes%d" % h, bufs=4, align_bytes=256)
                scales[c, h] = work.tile([P, 512], U8, name="scales%d" % h, bufs=4, align_bytes=256)
            nt = 4 if c < 3 else 2
            nc.scalar.activation(
                out=flat[c, h][:, t, x0:x1].rearrange("k (x i p) -> k x i p", i=nt, p=P),
                in_=acc[:, 0 : x1 - x0].rearrange("k (x p i) -> k x i p", i=nt, p=P),
                func=ACT.Square,
                scale=rts[:, h, t : t + 1],
            )

        def mix(engine_copy, c, h, j0, j1):
            cols = slice(128 * j0, 128 * j1)
            engine_copy(
                out=mixed[c, h][:, cols, :],
                in_=flat[c, h][:, :, cols].rearrange("k t m -> k m t"),
            )

        def ma(c, h, j):
            mix(nc.scalar.copy, c, h, j, j + 1)

        def mv(c, h, j0, j1):
            mix(nc.vector.tensor_copy, c, h, j0, j1)

        def q(c, h, j0, j1):
            cols = slice(128 * j0, 128 * j1)
            nc.vector.quantize_mx(
                out=codes[c, h][:, cols].bitcast(FP8X4),
                scales=scales[c, h][:, cols],
                in_=mixed[c, h][:, cols, :].rearrange("k m t -> k (m t)"),
            )

        def stage2_pass(c, j, h):
            if h == 0:
                ys[c, j] = ps2.tile([P, D], F32, name="y")
            cols = slice(128 * j, 128 * j + 128)
            nc.tensor.matmul_mx(
                out=ys[c, j][:],
                lhsT=codes[c, h][:, cols].bitcast(FP8X4),
                lhsT_scale=scales[c, h][:, cols],
                rhs=c_cod[:, h, :].bitcast(FP8X4),
                rhs_scale=c_scl[:, h, :],
                start=(h == 0),
                stop=(h == HALVES - 1),
            )

        def p2a(c, j):
            stage2_pass(c, j, 0)

        def p2b(c, j):
            stage2_pass(c, j, 1)

        def out_cols(c, j, d0, d1):
            res = work.tile([P, D], F32, name="res", bufs=6, align_bytes=64)
            nc.vector.scalar_tensor_tensor(
                out=res[:, d0:d1], in0=ys[c, j][:, d0:d1], scalar=ivpf[:, 4 * c + j : 4 * c + j + 1],
                in1=bas[:, d0:d1], op0=ALU.mult, op1=ALU.add,
            )
            if c < 3:
                rows = out[512 * c : 512 * c + 512, :].rearrange("(p i) d -> i p d", i=4)[j]
            else:
                x = 512 * c + 256 * (j // 2)
                rows = out[x : x + 256, :].rearrange("(p i) d -> i p d", i=2)[j % 2]
            nc.sync.dma_start(out=rows[:, d0:d1], in_=res[:, d0:d1])

        def out_tile(c, j):
            out_cols(c, j, 0, D)

        def s2(c, j):
            p2a(c, j)
            p2b(c, j)
            out_tile(c, j)

        def widen():
            nc.vector.tensor_copy(out=ivpf[:, 0:12], in_=ivp[:, 0:12])
            nc.vector.tensor_copy(out=ivpf[:, 12:16], in_=ivq[:, 0:4])

        first = [(0, 0), (0, 1), (1, 0), (1, 1)] + [(c, s) for s in range(2, 8) for c in (0, 1)]
        groups = [(c, s // 4, s % 4, 0, 512) for c, s in first]
        groups += [(2, s // 4, s % 4, 0, 512) for s in range(8)]
        groups += [(3, 0, t, 0, 512) for t in range(4)]
        groups += [(3, 1, t, x, x + 256) for x in (0, 256) for t in range(4)]
        after = {
            7: [(ma, 0, 0, 2)],
            8: [(ma, 0, 0, 3), (mv, 0, 0, 0, 2)],
            9: [(ma, 1, 0, 2)],
            10: [(ma, 1, 0, 3), (mv, 1, 0, 0, 2)],
            11: [(q, 0, 0, 0, 4)],
            12: [(q, 1, 0, 0, 4)],
            15: [(ma, 0, 1, 3), (mv, 0, 1, 0, 3)],
            16: [(ma, 1, 1, 3), (widen,)],
            17: [(q, 0, 1, 0, 4), (mv, 1, 1, 0, 3)],
            18: [(q, 1, 1, 0, 4)],
            19: [(s2, 0, 0), (s2, 0, 1), (ma, 2, 0, 2)],
            20: [(mv, 2, 0, 0, 2), (ma, 2, 0, 3), (s2, 0, 2)],
            21: [(s2, 0, 3)],
            22: [(q, 2, 0, 0, 4), (s2, 1, 0)],
            23: [(s2, 1, 1), (ma, 2, 1, 2)],
            24: [(mv, 2, 1, 0, 2), (ma, 2, 1, 3), (s2, 1, 2)],
            25: [(q, 2, 1, 0, 4), (s2, 1, 3)],
            26: [(s2, 2, 0)],
            27: [(ma, 3, 0, 2)],
            28: [(mv, 3, 0, 0, 2), (ma, 3, 0, 3)],
            29: [(s2, 2, 1)],
            30: [(q, 3, 0, 0, 4)],
            31: [(s2, 2, 2)],
            32: [(mv, 3, 1, 0, 2)],
            33: [(s2, 2, 3)],
            34: [(q, 3, 1, 0, 2)],
            35: [
                (ma, 3, 1, 3), (mv, 3, 1, 2, 3),
                (p2a, 3, 0), (p2b, 3, 0), (p2a, 3, 1), (p2b, 3, 1), (p2a, 3, 2), (p2a, 3, 3),
                (out_tile, 3, 0), (q, 3, 1, 2, 3), (p2b, 3, 2), (q, 3, 1, 3, 4), (p2b, 3, 3),
                (out_tile, 3, 1), (out_tile, 3, 2), (out_cols, 3, 3, 0, 256), (out_cols, 3, 3, 256, 512),
            ],
        }
        permute(0, 0)
        for n in range(3):
            warm_up()
        for h in range(HALVES):
            for t in range(4):
                if (h, t) != (0, 0):
                    permute(h, t)
        for n, group in enumerate(groups):
            stage1(*group)
            for step in after.get(n, []):
                step[0](*step[1:])
